import numpy as np
import ml_dtypes


def mxq(x, axis, fmt="e4m3"):
    dtype, down = {"e4m3": (ml_dtypes.float8_e4m3fn, 7), "e5m2": (ml_dtypes.float8_e5m2, 14)}[fmt]
    v = np.moveaxis(np.asarray(x, np.float32).astype(ml_dtypes.bfloat16).astype(np.float64), axis, -1)
    blocks = v.reshape(v.shape[:-1] + (-1, 32))
    amax = np.abs(blocks).max(-1, keepdims=True)
    byte = np.maximum(np.where(amax > 0, np.frexp(amax)[1] - 1 + 127, 0) - down, 1)
    scale = np.exp2(byte - 127.0)
    codes = (blocks / scale).astype(np.float32).astype(dtype).astype(np.float64)
    return np.moveaxis((codes * scale).reshape(v.shape), -1, axis)


WIDE = False


def mx_kscale(k):
    if not WIDE:
        return np.ones(k)
    levels = np.array([10, -10, 5, -5, 0])
    if k % 512:
        return np.exp2(np.random.permutation(np.resize(levels, k // 32))).repeat(32)
    a = np.empty((k // 512, 16))
    for p in range(k // 512):
        a[p, :8] = np.random.permutation(np.resize(levels, 8))
        for g in range(8):
            far = levels[np.abs(levels - a[p, g]) >= 10]
            a[p, g + 8] = far[np.random.randint(len(far))]
    return np.exp2(a.ravel()).repeat(32)


def f64(x):
    return np.asarray(x).astype(np.float64)


E2M1 = np.array([0.0, 0.5, 1.0, 1.5, 2.0, 3.0, 4.0, 6.0, -0.0, -0.5, -1.0, -1.5, -2.0, -3.0, -4.0, -6.0])


def pack_weight(w, fmt):
    k, n = w.shape
    w = f64(np.asarray(w, np.float32).astype(ml_dtypes.bfloat16)).reshape(k // 32, 32, n)
    amax = np.abs(w).max(1)
    if fmt == "e4m3":
        byte = np.frexp(amax)[1] - 1 + 127 - 7
    else:
        mant, ex = np.frexp(amax / 6.0)
        byte = np.where(mant > 0.5, ex, ex - 1) + 127
    byte = np.clip(np.where(amax > 0, byte, 1), 1, 254)
    scaled = (w * np.exp2(127.0 - byte)[:, None, :]).reshape(k, n).astype(np.float32)
    by_word = np.ascontiguousarray(scaled.reshape(k // 512, 128, 4, n).transpose(0, 1, 3, 2))
    if fmt == "e4m3":
        words = by_word.astype(ml_dtypes.float8_e4m3fn).view(np.uint8)
    else:
        c = by_word.astype(ml_dtypes.float4_e2m1fn).view(np.uint8) & 0xF
        words = (c[..., 0::2] | (c[..., 1::2] << 4)).reshape(k // 512, 128, 2 * n)
    return np.ascontiguousarray(words), np.ascontiguousarray(byte.astype(np.uint8).reshape(k // 512, 16, n))


def unpack_weight(words, scales, fmt):
    g, _, n = scales.shape
    words = np.ascontiguousarray(words).reshape(g, 128, n, -1)
    if fmt == "e4m3":
        vals = words.view(ml_dtypes.float8_e4m3fn).astype(np.float64)
    else:
        nib = np.empty((g, 128, n, 4), np.uint8)
        nib[..., 0::2] = words & 0xF
        nib[..., 1::2] = words >> 4
        vals = E2M1[nib]
    vals = vals * np.repeat(np.exp2(scales.astype(np.float64) - 127.0), 8, axis=1)[..., None]
    return vals.transpose(0, 1, 3, 2).reshape(g * 512, n)


D, K, M, T = 64, 1024, 512, 1024


def setup_inputs():
    n = np.random.standard_normal
    s = mx_kscale(K)[:, None]
    p_w0 = pack_weight(n((K, M)) / np.sqrt(K) / s, "e2m1")
    p_w1 = pack_weight(n((K, M)) / np.sqrt(K) / s, "e4m3")
    return {
        "x": (n((K, T + 2 * D)) * s).astype(np.float32),
        "w0_words": p_w0[0],
        "w0_scales": p_w0[1],
        "w1_words": p_w1[0],
        "w1_scales": p_w1[1],
        "w2": (n((K, M)) / np.sqrt(K) / s).astype(np.float32),
        "b": (0.3 * n(512)).astype(np.float32),
    }


def reference(x, w0_words, w0_scales, w1_words, w1_scales, w2, b):
    x_ = mxq(f64(x), 0, "e4m3")
    w0_ = unpack_weight(w0_words, w0_scales, "e2m1")
    w1_ = unpack_weight(w1_words, w1_scales, "e4m3")
    w2_ = mxq(f64(w2), 0, "e4m3")
    y = w0_.T @ x_[:, :T] + w1_.T @ x_[:, D:D + T] + w2_.T @ x_[:, 2 * D:]
    return y + f64(b)[:, None]

@@ -1,0 +1,186 @@
+from contextlib import ExitStack
+
+import concourse.mybir as mybir
+from concourse.masks import make_identity
+
+D, K, M, T = 64, 1024, 512, 1024
+FLOPS = 2 * 3 * K * M * T
+
+F32 = mybir.dt.float32
+BF16 = mybir.dt.bfloat16
+I32 = mybir.dt.int32
+U32 = mybir.dt.uint32
+U8 = mybir.dt.uint8
+FP8X4 = mybir.dt.float8_e4m3fn_x4
+FP4X4 = mybir.dt.float4_e2m1fn_x4
+IDENTITY = mybir.ActivationFunctionType.Identity
+
+P = 128
+PACK = 4
+K_PASS = P * PACK
+PASSES = K // K_PASS
+BANK = 512
+HALVES = T // BANK
+M_TILES = M // P
+X_COLS = T + 2 * D
+WINDOW = 256
+SCALAR_X_COLS = 128
+SCALAR_W_COLS = 64
+SHARED_W_PIECES = 5
+
+
+def tile_mix_dconv_fm_bias_kernel(tc, x, w0_words, w0_scales, w1_words, w1_scales, w2, b, out):
+    nc = tc.nc
+
+    with ExitStack() as ctx:
+        sb = ctx.enter_context(tc.tile_pool(name="sb", bufs=1))
+        psum = ctx.enter_context(tc.psum_pool(name="psum", bufs=1))
+        ctx.enter_context(tc.manual_schedule())
+
+        def load_rows(src, a, lo, hi, name):
+            raw = sb.tile([P, PACK, hi - lo], F32, name=name)
+            rows = src[a * K_PASS : (a + 1) * K_PASS, lo:hi]
+            nc.sync.dma_start(out=raw[:], in_=rows.rearrange("(p j) w -> p j w", j=PACK))
+            return raw
+
+        def interleave(copy, grouped, raw, lo, hi):
+            copy(
+                out=grouped[:, PACK * lo : PACK * hi].rearrange("p (c i j) -> p c j i", i=4, j=PACK),
+                in_=raw[:, :, lo:hi].rearrange("p j (c i) -> p c j i", i=4),
+            )
+
+        def quantize(codes, scales, at, grouped, lo, hi):
+            nc.vector.quantize_mx(
+                out=codes[:, at + lo : at + hi].bitcast(FP8X4),
+                scales=scales[:, at + lo : at + hi],
+                in_=grouped[:, PACK * lo : PACK * hi],
+            )
+
+        w1_plane = sb.tile([P, PASSES * M], U8, align_bytes=64)
+        w0_plane = sb.tile([P, PASSES * M], U8, align_bytes=64)
+        bias_rows = sb.tile([P, P], F32)
+        ident = sb.tile([P, P], F32)
+        nc.vector.memset(w1_plane[:].bitcast(I32), 0)
+        nc.vector.memset(bias_rows[:], 0.0)
+        nc.vector.memset(w0_plane[:].bitcast(I32), 0)
+        nc.vector.memset(ident[:], 0.0)
+        nc.gpsimd.dma_start(out=bias_rows[0:M_TILES, :], in_=b.rearrange("(m p) -> m p", p=P))
+        make_identity(nc, ident[:], nomemset=True)
+
+        def load_scales(plane, scales):
+            for quad in range(4):
+                nc.sync.dma_start(
+                    out=plane[32 * quad : 32 * quad + 4, :].bitcast(I32).rearrange("r (a n) -> r a n", a=PASSES),
+                    in_=scales[:, 4 * quad : 4 * quad + 4, :].bitcast(I32).rearrange("a r n -> r a n"),
+                )
+
+        edges = [0] + [D + WINDOW * (i + 1) for i in range(T // WINDOW - 1)] + [X_COLS]
+        x_order = [(a, 2 * h + i) for h in range(HALVES) for a in range(PASSES) for i in range(2)]
+        w_order = [(a, m) for m in range(M_TILES) for a in range(PASSES)]
+        x_raw = {}
+        w1_codes = sb.tile([P, PASSES * M], I32, align_bytes=64)
+        w0_codes = sb.tile([P, PASSES * 2 * M], U8, align_bytes=64)
+        for n, (a, i) in enumerate(x_order):
+            x_raw[a, i] = load_rows(x, a, edges[i], edges[i + 1], "x_raw%d_%d" % (a, i))
+            if n == 0:
+                load_scales(w1_plane, w1_scales)
+                nc.sync.dma_start(
+                    out=w1_codes[:].rearrange("p (a n) -> p a n", a=PASSES),
+                    in_=w1_words.rearrange("a p n i -> p a (n i)").bitcast(I32),
+                )
+            if n == 2:
+                nc.sync.dma_start(
+                    out=w0_codes[:].bitcast(I32).rearrange("p (a n) -> p a n", a=PASSES),
+                    in_=w0_words.rearrange("a p n -> p a n").bitcast(I32),
+                )
+                load_scales(w0_plane, w0_scales)
+        w2_raw = {}
+        for a, m in w_order:
+            w2_raw[a, m] = load_rows(w2, a, m * P, (m + 1) * P, "w2_raw%d_%d" % (a, m))
+
+        bias = sb.tile([P, M_TILES], F32)
+
+        def spread_bias():
+            bias_t = psum.tile([P, BANK], F32, tag="acc%d_%d" % (M_TILES - 1, HALVES - 1))
+            nc.tensor.transpose(bias_t[:, 0:P], bias_rows[:], ident[:])
+            nc.scalar.activation(out=bias[:], in_=bias_t[:, 0:M_TILES], func=IDENTITY)
+
+        acc = {}
+
+        def open_banks(h):
+            for m in range(M_TILES):
+                acc[m, h] = psum.tile([P, BANK], F32, name="acc%d_%d" % (m, h), tag="acc%d_%d" % (m, h))
+
+        x_codes = [sb.tile([P, X_COLS], U32, name="x_codes%d" % a, align_bytes=64) for a in range(PASSES)]
+        x_plane = [sb.tile([P, X_COLS], U8, name="x_plane%d" % a, align_bytes=64) for a in range(PASSES)]
+        w2_codes = sb.tile([P, PASSES * M], U32, align_bytes=64)
+        w2_plane = sb.tile([P, PASSES * M], U8, align_bytes=64)
+
+        def tap(lhsT, plane, shift, a, m, t0, width, start, stop):
+            h, lo = divmod(t0, BANK)
+            cols = slice(t0 + shift, t0 + shift + width)
+            nc.tensor.matmul_mx(
+                out=acc[m, h][:, lo : lo + width],
+                lhsT=lhsT,
+                lhsT_scale=plane[:, a * M + m * P : a * M + (m + 1) * P],
+                rhs=x_codes[a][:, cols].bitcast(FP8X4),
+                rhs_scale=x_plane[a][:, cols],
+                start=start,
+                stop=stop,
+            )
+
+        for a, i in x_order:
+            raw = x_raw[a, i]
+            at = edges[i]
+            width = edges[i + 1] - at
+            lo = D + WINDOW * i - at
+            hi = lo + WINDOW
+            rest = [(s, e) for s, e in ((0, lo), (hi, width)) if e > s]
+            grouped = sb.tile([P, PACK * width], BF16, name="x_bf%d_%d" % (a, i), align_bytes=64)
+            interleave(nc.scalar.copy, grouped, raw, lo, lo + SCALAR_X_COLS)
+            interleave(nc.vector.tensor_copy, grouped, raw, lo + SCALAR_X_COLS, hi)
+            for s, e in rest:
+                interleave(nc.vector.tensor_copy, grouped, raw, s, e)
+            quantize(x_codes[a], x_plane[a], at, grouped, lo, hi)
+            for s, e in rest:
+                quantize(x_codes[a], x_plane[a], at, grouped, s, e)
+            if a == 0 and i % 2 == 0:
+                open_banks(i // 2)
+            for m in range(M_TILES):
+                w = w1_codes[:, a * M + m * P : a * M + (m + 1) * P].bitcast(FP8X4)
+                tap(w, w1_plane, D, a, m, WINDOW * i, WINDOW, a == 0 and i % 2 == 0, False)
+            if (a, i) == (1, 0):
+                spread_bias()
+            if i % 2 == 1:
+                for m in range(M_TILES):
+                    w = w0_codes[:, 2 * (a * M + m * P) : 2 * (a * M + (m + 1) * P)].bitcast(FP4X4)
+                    tap(w, w0_plane, 0, a, m, BANK * (i // 2), BANK, False, False)
+
+        def finish(m):
+            result = sb.tile([P, T], F32, name="result%d" % m)
+            last = m == M_TILES - 1
+            for h in range(HALVES):
+                cols = slice(h * BANK, (h + 1) * BANK)
+                if last and h == HALVES - 1:
+                    nc.vector.tensor_scalar_add(out=result[:, cols], in0=acc[m, h][:], scalar1=bias[:, m : m + 1])
+                else:
+                    nc.scalar.activation(out=result[:, cols], in_=acc[m, h][:], func=IDENTITY, bias=bias[:, m : m + 1])
+                nc.sync.dma_start(out=out[m * P : (m + 1) * P, cols], in_=result[:, cols])
+
+        done = 0
+        for n, (a, m) in enumerate(w_order):
+            raw = w2_raw[a, m]
+            at = a * M + m * P
+            grouped = sb.tile([P, PACK * P], BF16, name="w2_bf%d_%d" % (a, m), align_bytes=64)
+            if n < SHARED_W_PIECES:
+                interleave(nc.scalar.copy, grouped, raw, 0, SCALAR_W_COLS)
+                interleave(nc.vector.tensor_copy, grouped, raw, SCALAR_W_COLS, P)
+            else:
+                interleave(nc.vector.tensor_copy, grouped, raw, 0, P)
+            quantize(w2_codes, w2_plane, at, grouped, 0, P)
+            for h in range(HALVES):
+                tap(w2_codes[:, at : at + P].bitcast(FP8X4), w2_plane, 2 * D, a, m, h * BANK, BANK, False, a == PASSES - 1)
+            if n >= SHARED_W_PIECES - 1:
+                while done < (n + 1) // PASSES:
+                    finish(done)
+                    done = done + 1

@@ -1,7 +1,6 @@
 from contextlib import ExitStack
 
 import concourse.mybir as mybir
-from concourse.masks import make_identity
 
 D, K, M, T = 64, 1024, 512, 1024
 FLOPS = 2 * 3 * K * M * T
@@ -24,9 +23,7 @@ HALVES = T // BANK
 M_TILES = M // P
 X_COLS = T + 2 * D
 WINDOW = 256
-SCALAR_X_COLS = 128
-SCALAR_W_COLS = 64
-SHARED_W_PIECES = 5
+W_COLS = 2 * P
 
 
 def tile_mix_dconv_fm_bias_kernel(tc, x, w0_words, w0_scales, w1_words, w1_scales, w2, b, out):
@@ -58,58 +55,53 @@ def tile_mix_dconv_fm_bias_kernel(tc, x, w0_words, w0_scales, w1_words, w1_scale
 
         w1_plane = sb.tile([P, PASSES * M], U8, align_bytes=64)
         w0_plane = sb.tile([P, PASSES * M], U8, align_bytes=64)
-        bias_rows = sb.tile([P, P], F32)
-        ident = sb.tile([P, P], F32)
+        bias_rows = sb.tile([P, P], F32, align_bytes=64)
+        bias = sb.tile([P, P], F32, align_bytes=64)
         nc.vector.memset(w1_plane[:].bitcast(I32), 0)
         nc.vector.memset(bias_rows[:], 0.0)
         nc.vector.memset(w0_plane[:].bitcast(I32), 0)
-        nc.vector.memset(ident[:], 0.0)
-        nc.gpsimd.dma_start(out=bias_rows[0:M_TILES, :], in_=b.rearrange("(m p) -> m p", p=P))
-        make_identity(nc, ident[:], nomemset=True)
 
-        def load_scales(plane, scales):
+        def load_scales(queue, plane, scales):
             for quad in range(4):
-                nc.sync.dma_start(
+                queue.dma_start(
                     out=plane[32 * quad : 32 * quad + 4, :].bitcast(I32).rearrange("r (a n) -> r a n", a=PASSES),
                     in_=scales[:, 4 * quad : 4 * quad + 4, :].bitcast(I32).rearrange("a r n -> r a n"),
                 )
 
-        edges = [0] + [D + WINDOW * (i + 1) for i in range(T // WINDOW - 1)] + [X_COLS]
-        x_order = [(a, 2 * h + i) for h in range(HALVES) for a in range(PASSES) for i in range(2)]
-        w_order = [(a, m) for m in range(M_TILES) for a in range(PASSES)]
-        x_raw = {}
+        nc.gpsimd.dma_start(
+            out=bias_rows[0:P:32, :].rearrange("q (m i) -> q m i", i=32),
+            in_=b.rearrange("(m q i) -> q m i", q=4, i=32),
+        )
+
+        split = BANK + 2 * D
+        x_span = [(0, split), (split, X_COLS)]
+        x_order = [(a, h) for a in range(PASSES) for h in range(HALVES)]
+        w_order = [(a, g) for g in range(M // W_COLS) for a in range(PASSES)]
         w1_codes = sb.tile([P, PASSES * M], I32, align_bytes=64)
         w0_codes = sb.tile([P, PASSES * 2 * M], U8, align_bytes=64)
-        for n, (a, i) in enumerate(x_order):
-            x_raw[a, i] = load_rows(x, a, edges[i], edges[i + 1], "x_raw%d_%d" % (a, i))
-            if n == 0:
-                load_scales(w1_plane, w1_scales)
+        x_raw = {}
+        for a, h in x_order:
+            x_raw[a, h] = load_rows(x, a, x_span[h][0], x_span[h][1], "x_raw%d_%d" % (a, h))
+            if (a, h) == (0, 0):
+                load_scales(nc.sync, w1_plane, w1_scales)
                 nc.sync.dma_start(
                     out=w1_codes[:].rearrange("p (a n) -> p a n", a=PASSES),
                     in_=w1_words.rearrange("a p n i -> p a (n i)").bitcast(I32),
                 )
-            if n == 2:
                 nc.sync.dma_start(
                     out=w0_codes[:].bitcast(I32).rearrange("p (a n) -> p a n", a=PASSES),
                     in_=w0_words.rearrange("a p n -> p a n").bitcast(I32),
                 )
-                load_scales(w0_plane, w0_scales)
+            if (a, h) == (0, 1):
+                load_scales(nc.sync, w0_plane, w0_scales)
         w2_raw = {}
-        for a, m in w_order:
-            w2_raw[a, m] = load_rows(w2, a, m * P, (m + 1) * P, "w2_raw%d_%d" % (a, m))
-
-        bias = sb.tile([P, M_TILES], F32)
-
-        def spread_bias():
-            bias_t = psum.tile([P, BANK], F32, tag="acc%d_%d" % (M_TILES - 1, HALVES - 1))
-            nc.tensor.transpose(bias_t[:, 0:P], bias_rows[:], ident[:])
-            nc.scalar.activation(out=bias[:], in_=bias_t[:, 0:M_TILES], func=IDENTITY)
+        for a, g in w_order:
+            w2_raw[a, g] = load_rows(w2, a, g * W_COLS, (g + 1) * W_COLS, "w2_raw%d_%d" % (a, g))
 
         acc = {}
-
-        def open_banks(h):
-            for m in range(M_TILES):
-                acc[m, h] = psum.tile([P, BANK], F32, name="acc%d_%d" % (m, h), tag="acc%d_%d" % (m, h))
+        for m in range(M_TILES):
+            for h in range(HALVES):
+                acc[m, h] = psum.tile([P, BANK], F32, name="acc%d_%d" % (m, h))
 
         x_codes = [sb.tile([P, X_COLS], U32, name="x_codes%d" % a, align_bytes=64) for a in range(PASSES)]
         x_plane = [sb.tile([P, X_COLS], U8, name="x_plane%d" % a, align_bytes=64) for a in range(PASSES)]
@@ -129,58 +121,74 @@ def tile_mix_dconv_fm_bias_kernel(tc, x, w0_words, w0_scales, w1_words, w1_scale
                 stop=stop,
             )
 
-        for a, i in x_order:
-            raw = x_raw[a, i]
-            at = edges[i]
-            width = edges[i + 1] - at
-            lo = D + WINDOW * i - at
-            hi = lo + WINDOW
-            rest = [(s, e) for s, e in ((0, lo), (hi, width)) if e > s]
-            grouped = sb.tile([P, PACK * width], BF16, name="x_bf%d_%d" % (a, i), align_bytes=64)
-            interleave(nc.scalar.copy, grouped, raw, lo, lo + SCALAR_X_COLS)
-            interleave(nc.vector.tensor_copy, grouped, raw, lo + SCALAR_X_COLS, hi)
-            for s, e in rest:
+        def tap0(a, h, m):
+            w = w0_codes[:, 2 * (a * M + m * P) : 2 * (a * M + (m + 1) * P)].bitcast(FP4X4)
+            tap(w, w0_plane, 0, a, m, BANK * h, BANK, False, False)
+
+        def tap1(a, h, i, m):
+            w = w1_codes[:, a * M + m * P : a * M + (m + 1) * P].bitcast(FP8X4)
+            tap(w, w1_plane, D, a, m, BANK * h + WINDOW * i, WINDOW, a == 0 and i == 0, False)
+
+        def tap2(a, m):
+            w = w2_codes[:, a * M + m * P : a * M + (m + 1) * P].bitcast(FP8X4)
+            for h in range(HALVES):
+                tap(w, w2_plane, 2 * D, a, m, BANK * h, BANK, False, a == PASSES - 1)
+
+        for a, h in x_order:
+            raw = x_raw[a, h]
+            at = x_span[h][0]
+            width = x_span[h][1] - at
+            grouped = sb.tile([P, PACK * width], BF16, name="x_bf%d_%d" % (a, h), align_bytes=64)
+            cut = width - WINDOW
+            vector_parts = [(s, min(s + WINDOW, cut)) for s in range(0, cut, WINDOW)]
+            interleave(nc.scalar.copy, grouped, raw, cut, width)
+            for s, e in vector_parts:
                 interleave(nc.vector.tensor_copy, grouped, raw, s, e)
-            quantize(x_codes[a], x_plane[a], at, grouped, lo, hi)
-            for s, e in rest:
+            for s, e in vector_parts + [(cut, width)]:
                 quantize(x_codes[a], x_plane[a], at, grouped, s, e)
-            if a == 0 and i % 2 == 0:
-                open_banks(i // 2)
+            if (a, h) == (0, 1):
+                nc.vector.transpose(bias[:], bias_rows[:])
             for m in range(M_TILES):
-                w = w1_codes[:, a * M + m * P : a * M + (m + 1) * P].bitcast(FP8X4)
-                tap(w, w1_plane, D, a, m, WINDOW * i, WINDOW, a == 0 and i % 2 == 0, False)
-            if (a, i) == (1, 0):
-                spread_bias()
-            if i % 2 == 1:
+                tap1(a, h, 0, m)
+            if (a, h) != x_order[-1]:
                 for m in range(M_TILES):
-                    w = w0_codes[:, 2 * (a * M + m * P) : 2 * (a * M + (m + 1) * P)].bitcast(FP4X4)
-                    tap(w, w0_plane, 0, a, m, BANK * (i // 2), BANK, False, False)
+                    tap1(a, h, 1, m)
+                for m in range(M_TILES):
+                    tap0(a, h, m)
 
-        def finish(m):
+        def late_taps(m):
+            tap1(PASSES - 1, HALVES - 1, 1, m)
+            tap0(PASSES - 1, HALVES - 1, m)
+
+        def finish(m, second):
             result = sb.tile([P, T], F32, name="result%d" % m)
-            last = m == M_TILES - 1
-            for h in range(HALVES):
-                cols = slice(h * BANK, (h + 1) * BANK)
-                if last and h == HALVES - 1:
-                    nc.vector.tensor_scalar_add(out=result[:, cols], in0=acc[m, h][:], scalar1=bias[:, m : m + 1])
-                else:
-                    nc.scalar.activation(out=result[:, cols], in_=acc[m, h][:], func=IDENTITY, bias=bias[:, m : m + 1])
-                nc.sync.dma_start(out=out[m * P : (m + 1) * P, cols], in_=result[:, cols])
-
-        done = 0
-        for n, (a, m) in enumerate(w_order):
-            raw = w2_raw[a, m]
-            at = a * M + m * P
-            grouped = sb.tile([P, PACK * P], BF16, name="w2_bf%d_%d" % (a, m), align_bytes=64)
-            if n < SHARED_W_PIECES:
-                interleave(nc.scalar.copy, grouped, raw, 0, SCALAR_W_COLS)
-                interleave(nc.vector.tensor_copy, grouped, raw, SCALAR_W_COLS, P)
+            rows = slice(m * P, (m + 1) * P)
+            shift = bias[:, 32 * m : 32 * m + 1]
+            nc.scalar.activation(out=result[:, 0:BANK], in_=acc[m, 0][:], func=IDENTITY, bias=shift)
+            if m == M_TILES - 1:
+                nc.sync.dma_start(out=out[rows, 0:BANK], in_=result[:, 0:BANK])
+            if second:
+                nc.vector.tensor_scalar_add(out=result[:, BANK:T], in0=acc[m, 1][:], scalar1=shift)
             else:
+                nc.scalar.activation(out=result[:, BANK:T], in_=acc[m, 1][:], func=IDENTITY, bias=shift)
+            if m == M_TILES - 1:
+                nc.sync.dma_start(out=out[rows, BANK:T], in_=result[:, BANK:T])
+            else:
+                nc.sync.dma_start(out=out[rows, :], in_=result[:])
+
+        late_taps(0)
+        for g in range(M // W_COLS):
+            for a in range(PASSES):
+                raw = w2_raw[a, g]
+                at = a * M + g * W_COLS
+                grouped = sb.tile([P, PACK * W_COLS], BF16, name="w2_bf%d_%d" % (a, g), align_bytes=64)
                 interleave(nc.vector.tensor_copy, grouped, raw, 0, P)
-            quantize(w2_codes, w2_plane, at, grouped, 0, P)
-            for h in range(HALVES):
-                tap(w2_codes[:, at : at + P].bitcast(FP8X4), w2_plane, 2 * D, a, m, h * BANK, BANK, False, a == PASSES - 1)
-            if n >= SHARED_W_PIECES - 1:
-                while done < (n + 1) // PASSES:
-                    finish(done)
-                    done = done + 1
+                interleave(nc.scalar.copy if g == 0 else nc.vector.tensor_copy, grouped, raw, P, W_COLS)
+                quantize(w2_codes, w2_plane, at, grouped, 0, P)
+                quantize(w2_codes, w2_plane, at, grouped, P, W_COLS)
+            for m in (2 * g, 2 * g + 1):
+                tap2(0, m)
+                if m + 1 < M_TILES:
+                    late_taps(m + 1)
+                tap2(1, m)
+                finish(m, g == 1)

from contextlib import ExitStack

import concourse.mybir as mybir

D, K, M, T = 64, 1024, 512, 1024
FLOPS = 2 * 3 * K * M * T

F32 = mybir.dt.float32
BF16 = mybir.dt.bfloat16
I32 = mybir.dt.int32
U32 = mybir.dt.uint32
U8 = mybir.dt.uint8
FP8X4 = mybir.dt.float8_e4m3fn_x4
FP4X4 = mybir.dt.float4_e2m1fn_x4
IDENTITY = mybir.ActivationFunctionType.Identity

P = 128
PACK = 4
K_PASS = P * PACK
PASSES = K // K_PASS
BANK = 512
HALVES = T // BANK
M_TILES = M // P
X_COLS = T + 2 * D
WINDOW = 256
W_COLS = 2 * P


def tile_mix_dconv_fm_bias_kernel(tc, x, w0_words, w0_scales, w1_words, w1_scales, w2, b, out):
    nc = tc.nc

    with ExitStack() as ctx:
        sb = ctx.enter_context(tc.tile_pool(name="sb", bufs=1))
        psum = ctx.enter_context(tc.psum_pool(name="psum", bufs=1))
        ctx.enter_context(tc.manual_schedule())

        def load_rows(src, a, lo, hi, name):
            raw = sb.tile([P, PACK, hi - lo], F32, name=name)
            rows = src[a * K_PASS : (a + 1) * K_PASS, lo:hi]
            nc.sync.dma_start(out=raw[:], in_=rows.rearrange("(p j) w -> p j w", j=PACK))
            return raw

        def interleave(copy, grouped, raw, lo, hi):
            copy(
                out=grouped[:, PACK * lo : PACK * hi].rearrange("p (c i j) -> p c j i", i=4, j=PACK),
                in_=raw[:, :, lo:hi].rearrange("p j (c i) -> p c j i", i=4),
            )

        def quantize(codes, scales, at, grouped, lo, hi):
            nc.vector.quantize_mx(
                out=codes[:, at + lo : at + hi].bitcast(FP8X4),
                scales=scales[:, at + lo : at + hi],
                in_=grouped[:, PACK * lo : PACK * hi],
            )

        w1_plane = sb.tile([P, PASSES * M], U8, align_bytes=64)
        w0_plane = sb.tile([P, PASSES * M], U8, align_bytes=64)
        bias_rows = sb.tile([P, P], F32, align_bytes=64)
        bias = sb.tile([P, P], F32, align_bytes=64)
        nc.vector.memset(w1_plane[:].bitcast(I32), 0)
        nc.vector.memset(bias_rows[:], 0.0)
        nc.vector.memset(w0_plane[:].bitcast(I32), 0)

        def load_scales(queue, plane, scales):
            for quad in range(4):
                queue.dma_start(
                    out=plane[32 * quad : 32 * quad + 4, :].bitcast(I32).rearrange("r (a n) -> r a n", a=PASSES),
                    in_=scales[:, 4 * quad : 4 * quad + 4, :].bitcast(I32).rearrange("a r n -> r a n"),
                )

        nc.gpsimd.dma_start(
            out=bias_rows[0:P:32, :].rearrange("q (m i) -> q m i", i=32),
            in_=b.rearrange("(m q i) -> q m i", q=4, i=32),
        )

        split = BANK + 2 * D
        x_span = [(0, split), (split, X_COLS)]
        x_order = [(a, h) for a in range(PASSES) for h in range(HALVES)]
        w_order = [(a, g) for g in range(M // W_COLS) for a in range(PASSES)]
        w1_codes = sb.tile([P, PASSES * M], I32, align_bytes=64)
        w0_codes = sb.tile([P, PASSES * 2 * M], U8, align_bytes=64)
        x_raw = {}
        for a, h in x_order:
            x_raw[a, h] = load_rows(x, a, x_span[h][0], x_span[h][1], "x_raw%d_%d" % (a, h))
            if (a, h) == (0, 0):
                load_scales(nc.sync, w1_plane, w1_scales)
                nc.sync.dma_start(
                    out=w1_codes[:].rearrange("p (a n) -> p a n", a=PASSES),
                    in_=w1_words.rearrange("a p n i -> p a (n i)").bitcast(I32),
                )
                nc.sync.dma_start(
                    out=w0_codes[:].bitcast(I32).rearrange("p (a n) -> p a n", a=PASSES),
                    in_=w0_words.rearrange("a p n -> p a n").bitcast(I32),
                )
            if (a, h) == (0, 1):
                load_scales(nc.sync, w0_plane, w0_scales)
        w2_raw = {}
        for a, g in w_order:
            w2_raw[a, g] = load_rows(w2, a, g * W_COLS, (g + 1) * W_COLS, "w2_raw%d_%d" % (a, g))

        acc = {}
        for m in range(M_TILES):
            for h in range(HALVES):
                acc[m, h] = psum.tile([P, BANK], F32, name="acc%d_%d" % (m, h))

        x_codes = [sb.tile([P, X_COLS], U32, name="x_codes%d" % a, align_bytes=64) for a in range(PASSES)]
        x_plane = [sb.tile([P, X_COLS], U8, name="x_plane%d" % a, align_bytes=64) for a in range(PASSES)]
        w2_codes = sb.tile([P, PASSES * M], U32, align_bytes=64)
        w2_plane = sb.tile([P, PASSES * M], U8, align_bytes=64)

        def tap(lhsT, plane, shift, a, m, t0, width, start, stop):
            h, lo = divmod(t0, BANK)
            cols = slice(t0 + shift, t0 + shift + width)
            nc.tensor.matmul_mx(
                out=acc[m, h][:, lo : lo + width],
                lhsT=lhsT,
                lhsT_scale=plane[:, a * M + m * P : a * M + (m + 1) * P],
                rhs=x_codes[a][:, cols].bitcast(FP8X4),
                rhs_scale=x_plane[a][:, cols],
                start=start,
                stop=stop,
            )

        def tap0(a, h, m):
            w = w0_codes[:, 2 * (a * M + m * P) : 2 * (a * M + (m + 1) * P)].bitcast(FP4X4)
            tap(w, w0_plane, 0, a, m, BANK * h, BANK, False, False)

        def tap1(a, h, i, m):
            w = w1_codes[:, a * M + m * P : a * M + (m + 1) * P].bitcast(FP8X4)
            tap(w, w1_plane, D, a, m, BANK * h + WINDOW * i, WINDOW, a == 0 and i == 0, False)

        def tap2(a, m):
            w = w2_codes[:, a * M + m * P : a * M + (m + 1) * P].bitcast(FP8X4)
            for h in range(HALVES):
                tap(w, w2_plane, 2 * D, a, m, BANK * h, BANK, False, a == PASSES - 1)

        for a, h in x_order:
            raw = x_raw[a, h]
            at = x_span[h][0]
            width = x_span[h][1] - at
            grouped = sb.tile([P, PACK * width], BF16, name="x_bf%d_%d" % (a, h), align_bytes=64)
            cut = width - WINDOW
            vector_parts = [(s, min(s + WINDOW, cut)) for s in range(0, cut, WINDOW)]
            interleave(nc.scalar.copy, grouped, raw, cut, width)
            for s, e in vector_parts:
                interleave(nc.vector.tensor_copy, grouped, raw, s, e)
            for s, e in vector_parts + [(cut, width)]:
                quantize(x_codes[a], x_plane[a], at, grouped, s, e)
            if (a, h) == (0, 1):
                nc.vector.transpose(bias[:], bias_rows[:])
            for m in range(M_TILES):
                tap1(a, h, 0, m)
            if (a, h) != x_order[-1]:
                for m in range(M_TILES):
                    tap1(a, h, 1, m)
                for m in range(M_TILES):
                    tap0(a, h, m)

        def late_taps(m):
            tap1(PASSES - 1, HALVES - 1, 1, m)
            tap0(PASSES - 1, HALVES - 1, m)

        def finish(m, second):
            result = sb.tile([P, T], F32, name="result%d" % m)
            rows = slice(m * P, (m + 1) * P)
            shift = bias[:, 32 * m : 32 * m + 1]
            nc.scalar.activation(out=result[:, 0:BANK], in_=acc[m, 0][:], func=IDENTITY, bias=shift)
            if m == M_TILES - 1:
                nc.sync.dma_start(out=out[rows, 0:BANK], in_=result[:, 0:BANK])
            if second:
                nc.vector.tensor_scalar_add(out=result[:, BANK:T], in0=acc[m, 1][:], scalar1=shift)
            else:
                nc.scalar.activation(out=result[:, BANK:T], in_=acc[m, 1][:], func=IDENTITY, bias=shift)
            if m == M_TILES - 1:
                nc.sync.dma_start(out=out[rows, BANK:T], in_=result[:, BANK:T])
            else:
                nc.sync.dma_start(out=out[rows, :], in_=result[:])

        late_taps(0)
        for g in range(M // W_COLS):
            for a in range(PASSES):
                raw = w2_raw[a, g]
                at = a * M + g * W_COLS
                grouped = sb.tile([P, PACK * W_COLS], BF16, name="w2_bf%d_%d" % (a, g), align_bytes=64)
                interleave(nc.vector.tensor_copy, grouped, raw, 0, P)
                interleave(nc.scalar.copy if g == 0 else nc.vector.tensor_copy, grouped, raw, P, W_COLS)
                quantize(w2_codes, w2_plane, at, grouped, 0, P)
                quantize(w2_codes, w2_plane, at, grouped, P, W_COLS)
            for m in (2 * g, 2 * g + 1):
                tap2(0, m)
                if m + 1 < M_TILES:
                    late_taps(m + 1)
                tap2(1, m)
                finish(m, g == 1)
